import numpy as np
import ml_dtypes


def mxq(x, axis, fmt="e4m3"):
    dtype, down = {"e4m3": (ml_dtypes.float8_e4m3fn, 7), "e5m2": (ml_dtypes.float8_e5m2, 14)}[fmt]
    v = np.moveaxis(np.asarray(x, np.float32).astype(ml_dtypes.bfloat16).astype(np.float64), axis, -1)
    blocks = v.reshape(v.shape[:-1] + (-1, 32))
    amax = np.abs(blocks).max(-1, keepdims=True)
    byte = np.maximum(np.where(amax > 0, np.frexp(amax)[1] - 1 + 127, 0) - down, 1)
    scale = np.exp2(byte - 127.0)
    codes = (blocks / scale).astype(np.float32).astype(dtype).astype(np.float64)
    return np.moveaxis((codes * scale).reshape(v.shape), -1, axis)


WIDE = False


def mx_kscale(k):
    if not WIDE:
        return np.ones(k)
    levels = np.array([30, -30])
    if k % 512:
        return np.exp2(np.random.permutation(np.resize(levels, k // 32))).repeat(32)
    a = np.empty((k // 512, 16))
    for p in range(k // 512):
        a[p, :8] = np.random.permutation(np.resize(levels, 8))
        for g in range(8):
            far = levels[np.abs(levels - a[p, g]) >= 10]
            a[p, g + 8] = far[np.random.randint(len(far))]
    return np.exp2(a.ravel()).repeat(32)


def f64(x):
    return np.asarray(x).astype(np.float64)


def striped(idx):
    return np.tile(idx.reshape(-1, 16).T, (8, 1)).astype(np.uint16)


def unstriped(offs):
    return offs[:16].T.reshape(-1).astype(np.int64)


E2M1 = np.array([0.0, 0.5, 1.0, 1.5, 2.0, 3.0, 4.0, 6.0, -0.0, -0.5, -1.0, -1.5, -2.0, -3.0, -4.0, -6.0])


def pack_weight(w, fmt):
    k, n = w.shape
    w = f64(np.asarray(w, np.float32).astype(ml_dtypes.bfloat16)).reshape(k // 32, 32, n)
    amax = np.abs(w).max(1)
    if fmt == "e4m3":
        byte = np.frexp(amax)[1] - 1 + 127 - 7
    else:
        mant, ex = np.frexp(amax / 6.0)
        byte = np.where(mant > 0.5, ex, ex - 1) + 127
    byte = np.clip(np.where(amax > 0, byte, 1), 1, 254)
    scaled = (w * np.exp2(127.0 - byte)[:, None, :]).reshape(k, n).astype(np.float32)
    by_word = np.ascontiguousarray(scaled.reshape(k // 512, 128, 4, n).transpose(0, 1, 3, 2))
    if fmt == "e4m3":
        words = by_word.astype(ml_dtypes.float8_e4m3fn).view(np.uint8)
    else:
        c = by_word.astype(ml_dtypes.float4_e2m1fn).view(np.uint8) & 0xF
        words = (c[..., 0::2] | (c[..., 1::2] << 4)).reshape(k // 512, 128, 2 * n)
    return np.ascontiguousarray(words), np.ascontiguousarray(byte.astype(np.uint8).reshape(k // 512, 16, n))


def unpack_weight(words, scales, fmt):
    g, _, n = scales.shape
    words = np.ascontiguousarray(words).reshape(g, 128, n, -1)
    if fmt == "e4m3":
        vals = words.view(ml_dtypes.float8_e4m3fn).astype(np.float64)
    else:
        nib = np.empty((g, 128, n, 4), np.uint8)
        nib[..., 0::2] = words & 0xF
        nib[..., 1::2] = words >> 4
        vals = E2M1[nib]
    vals = vals * np.repeat(np.exp2(scales.astype(np.float64) - 127.0), 8, axis=1)[..., None]
    return vals.transpose(0, 1, 3, 2).reshape(g * 512, n)


K, T, E, C, N = 384, 2048, 4, 512, 1024


def by_expert(wq, xq):
    return np.concatenate([wq[e].T @ xq[:, e * C:(e + 1) * C] for e in range(E)], axis=1)


def setup_inputs():
    n = np.random.standard_normal
    s = mx_kscale(N)[:, None]
    w = [pack_weight(m, "e2m1") for m in n((E, N, K)) / np.sqrt(N) / s[None]]
    return {
        "dyT": (n((N, T)) * s).astype(np.float32),
        "w_words": np.stack([m[0] for m in w]),
        "w_scales": np.stack([m[1] for m in w]),
        "gate": np.tile(np.random.uniform(0.2, 1.0, E * C), (N, 1)).astype(np.float32),
        "offs": striped(np.random.permutation(T)[:E * C]),
    }


def reference(dyT, w_words, w_scales, gate, offs):
    idx = unstriped(offs)
    w = np.stack([unpack_weight(w_words[e], w_scales[e], "e2m1") for e in range(E)])
    gq = mxq(f64(gate) * f64(dyT)[:, idx], 0, "e5m2")
    dx = by_expert(w, gq)
    out = np.zeros((K, T))
    out[:, idx] = dx
    return out

@@ -1,0 +1,164 @@
+from contextlib import ExitStack
+
+import concourse.mybir as mybir
+
+K, T, E, C, N = 384, 2048, 4, 512, 1024
+FLOPS = 2 * K * N * E * C
+BYTES = 4 * N * T + 2 * E * N * K // 4 + E * N // 32 * K + 4 * T + 2 * 128 * T // 16 + 4 * K * T
+
+F32 = mybir.dt.float32
+BF16 = mybir.dt.bfloat16
+I32 = mybir.dt.int32
+U32 = mybir.dt.uint32
+U16 = mybir.dt.uint16
+U8 = mybir.dt.uint8
+FP8X4 = mybir.dt.float8_e5m2_x4
+FP4X4 = mybir.dt.float4_e2m1fn_x4
+MULT = mybir.AluOpType.mult
+
+P = 128
+PACK = 4
+PASSES = N // (P * PACK)
+KT = K // P
+GROUPS = E * PASSES
+PAIR = 2 * C
+PAIRS = E // 2
+
+
+def tile_moe_bdx_lin_none_kernel(tc, dyT, w_words, w_scales, gate, offs, out):
+    nc = tc.nc
+    with ExitStack() as ctx:
+        held = ctx.enter_context(tc.tile_pool(name="held", bufs=1))
+        gath = ctx.enter_context(tc.tile_pool(name="gath", bufs=3))
+        psum = ctx.enter_context(tc.psum_pool(name="psum", bufs=8))
+
+        offsets = held.tile([P, T // 16], U16, name="offsets")
+        gates = held.tile([P, T], F32, name="gates")
+        dy = [[held.tile([P, T], F32, name=f"dy{a}{t}") for t in range(PACK)] for a in range(PASSES)]
+        words = held.tile([P, GROUPS * 2 * K], U8, name="words", align_bytes=64)
+        wplanes = held.tile([P, GROUPS * K], U8, name="wplanes", align_bytes=64)
+        outs = [held.tile([P, T], F32, name=f"outs{kt}") for kt in range(KT)]
+        codes = [held.tile([P, T], U32, name=f"codes{a}", align_bytes=64) for a in range(PASSES)]
+        planes = [held.tile([P, T], U8, name=f"planes{a}", align_bytes=64) for a in range(PASSES)]
+
+        dy_rows = dyT.rearrange("(a p t) c -> a t p c", a=PASSES, p=P, t=PACK)
+
+        nc.vector.memset(wplanes[:].bitcast(I32), 0)
+
+        nc.sync.dma_start(offsets[:], offs)
+        nc.sync.dma_start(gates[:, 0:C], gate[0:P, 0:C])
+        nc.sync.dma_start(dy[0][0][:], dy_rows[0, 0])
+        nc.sync.dma_start(gates[:, C:PAIR], gate[0:P, C:PAIR])
+        nc.sync.dma_start(gates[:, PAIR:T], gate[0:P, PAIR:T])
+        for a in range(PASSES):
+            for t in range(PACK):
+                if a + t > 0:
+                    nc.sync.dma_start(dy[a][t][:], dy_rows[a, t])
+        nc.sync.dma_start(
+            words[:].bitcast(I32).rearrange("p (g b) -> p g b", g=GROUPS),
+            w_words.bitcast(I32).rearrange("e a p b -> p (e a) b"),
+        )
+        for q in range(4):
+            nc.sync.dma_start(
+                wplanes[32 * q : 32 * q + 4, :].bitcast(I32).rearrange("p (g k) -> p g k", g=GROUPS),
+                w_scales.bitcast(I32).rearrange("e a f k -> f (e a) k")[4 * q : 4 * q + 4, :, :],
+            )
+
+        def gather(g4, a, t, pair, lo, hi):
+            s0 = pair * PAIR + lo
+            s1 = pair * PAIR + hi
+            nc.vector.tensor_tensor(
+                g4[:, t, lo:hi],
+                dy[a][t][:].indirect(offsets[:, s0 // 16 : s1 // 16]),
+                gates[:, s0:s1],
+                MULT,
+            )
+
+        def interleave(g4, half):
+            grouped = gath.tile([P, C, PACK], BF16, name="grouped", bufs=4, align_bytes=64)
+            nc.scalar.copy(grouped[:], g4[:, :, half * C : (half + 1) * C].rearrange("p t n -> p n t"))
+            return grouped
+
+        def quantise(grouped, a, e):
+            cols = slice(e * C, (e + 1) * C)
+            nc.vector.quantize_mx(
+                out=codes[a][:, cols].bitcast(FP8X4),
+                scales=planes[a][:, cols],
+                in_=grouped[:].rearrange("p n t -> p (n t)"),
+            )
+
+        def new_g4():
+            g4 = gath.tile([P, PACK, PAIR], F32, name="g4")
+            return g4
+
+        def products(pair):
+            ys = []
+            for kt in range(KT):
+                y = held.tile([P, PAIR], F32, name=f"y{pair}{kt}")
+                ys.append(y)
+                for half in range(2):
+                    e = 2 * pair + half
+                    cols = slice(e * C, (e + 1) * C)
+                    acc = psum.tile([P, C], F32, name="acc")
+                    for a in range(PASSES):
+                        w0 = (e * PASSES + a) * K + P * kt
+                        nc.tensor.matmul_mx(
+                            out=acc[:],
+                            lhsT=words[:, 2 * w0 : 2 * (w0 + P)].bitcast(FP4X4),
+                            lhsT_scale=wplanes[:, w0 : w0 + P],
+                            rhs=codes[a][:, cols].bitcast(FP8X4),
+                            rhs_scale=planes[a][:, cols],
+                            start=(a == 0),
+                            stop=(a == PASSES - 1),
+                        )
+                    nc.scalar.copy(y[:, half * C : (half + 1) * C], acc[:])
+            return ys
+
+        def scatter(ys, pair, kt):
+            nc.vector.tensor_copy(
+                outs[kt][:].indirect(offsets[:, pair * PAIR // 16 : (pair + 1) * PAIR // 16]), ys[kt][:]
+            )
+
+        g00 = new_g4()
+        g01 = new_g4()
+        gather(g00, 0, 0, 0, 0, C)
+        gather(g00, 0, 0, 0, C, PAIR)
+        gather(g01, 0, 0, 1, 0, PAIR)
+        for t in range(1, PACK):
+            gather(g00, 0, t, 0, 0, PAIR)
+            gather(g01, 0, t, 1, 0, PAIR)
+        b00 = [interleave(g00, h) for h in range(2)]
+        b01 = [interleave(g01, h) for h in range(2)]
+
+        g10 = new_g4()
+        gather(g10, 1, 0, 0, 0, PAIR)
+        gather(g10, 1, 1, 0, 0, PAIR)
+        for h in range(2):
+            quantise(b00[h], 0, h)
+        gather(g10, 1, 2, 0, 0, PAIR)
+        gather(g10, 1, 3, 0, 0, PAIR)
+        for h in range(2):
+            quantise(b01[h], 0, 2 + h)
+        b10 = [interleave(g10, h) for h in range(2)]
+
+        g11 = new_g4()
+        gather(g11, 1, 0, 1, 0, PAIR)
+        gather(g11, 1, 1, 1, 0, PAIR)
+        gather(g11, 1, 2, 1, 0, PAIR)
+        for h in range(2):
+            quantise(b10[h], 1, h)
+        gather(g11, 1, 3, 1, 0, PAIR)
+        y0 = products(0)
+        b11 = [interleave(g11, h) for h in range(2)]
+
+        scatter(y0, 0, 0)
+        scatter(y0, 0, 1)
+        for h in range(2):
+            quantise(b11[h], 1, 2 + h)
+        y1 = products(1)
+        scatter(y0, 0, 2)
+        for kt in range(KT):
+            scatter(y1, 1, kt)
+            rows = slice(kt * P, (kt + 1) * P)
+            nc.sync.dma_start(out[rows, 0:PAIR], outs[kt][:, 0:PAIR])
+            nc.scalar.dma_start(out[rows, PAIR:T], outs[kt][:, PAIR:T])

@@ -22,6 +22,7 @@ PASSES = N // (P * PACK)
 KT = K // P
 GROUPS = E * PASSES
 PAIR = 2 * C
+FIRST = 256
 PAIRS = E // 2
 
 
@@ -46,9 +47,9 @@ def tile_moe_bdx_lin_none_kernel(tc, dyT, w_words, w_scales, gate, offs, out):
         nc.vector.memset(wplanes[:].bitcast(I32), 0)
 
         nc.sync.dma_start(offsets[:], offs)
-        nc.sync.dma_start(gates[:, 0:C], gate[0:P, 0:C])
+        nc.sync.dma_start(gates[:, 0:FIRST], gate[0:P, 0:FIRST])
         nc.sync.dma_start(dy[0][0][:], dy_rows[0, 0])
-        nc.sync.dma_start(gates[:, C:PAIR], gate[0:P, C:PAIR])
+        nc.sync.dma_start(gates[:, FIRST:PAIR], gate[0:P, FIRST:PAIR])
         nc.sync.dma_start(gates[:, PAIR:T], gate[0:P, PAIR:T])
         for a in range(PASSES):
             for t in range(PACK):
@@ -74,13 +75,18 @@ def tile_moe_bdx_lin_none_kernel(tc, dyT, w_words, w_scales, gate, offs, out):
                 MULT,
             )
 
-        def interleave(g4, half):
-            grouped = gath.tile([P, C, PACK], BF16, name="grouped", bufs=4, align_bytes=64)
-            nc.scalar.copy(grouped[:], g4[:, :, half * C : (half + 1) * C].rearrange("p t n -> p n t"))
+        def interleave(g4):
+            grouped = gath.tile([P, PAIR, PACK], BF16, name="grouped", bufs=3, align_bytes=64)
+            for half in range(2):
+                cols = slice(half * C, (half + 1) * C)
+                nc.scalar.copy(
+                    grouped[:, cols, :].rearrange("p (c i) t -> p c t i", i=4),
+                    g4[:, :, cols].rearrange("p t (c i) -> p c t i", i=4),
+                )
             return grouped
 
-        def quantise(grouped, a, e):
-            cols = slice(e * C, (e + 1) * C)
+        def quantise(grouped, a, pair):
+            cols = slice(pair * PAIR, (pair + 1) * PAIR)
             nc.vector.quantize_mx(
                 out=codes[a][:, cols].bitcast(FP8X4),
                 scales=planes[a][:, cols],
@@ -121,40 +127,36 @@ def tile_moe_bdx_lin_none_kernel(tc, dyT, w_words, w_scales, gate, offs, out):
 
         g00 = new_g4()
         g01 = new_g4()
-        gather(g00, 0, 0, 0, 0, C)
-        gather(g00, 0, 0, 0, C, PAIR)
+        gather(g00, 0, 0, 0, 0, FIRST)
+        gather(g00, 0, 0, 0, FIRST, PAIR)
         gather(g01, 0, 0, 1, 0, PAIR)
         for t in range(1, PACK):
             gather(g00, 0, t, 0, 0, PAIR)
             gather(g01, 0, t, 1, 0, PAIR)
-        b00 = [interleave(g00, h) for h in range(2)]
-        b01 = [interleave(g01, h) for h in range(2)]
+        b00 = interleave(g00)
+        b01 = interleave(g01)
 
         g10 = new_g4()
         gather(g10, 1, 0, 0, 0, PAIR)
         gather(g10, 1, 1, 0, 0, PAIR)
-        for h in range(2):
-            quantise(b00[h], 0, h)
         gather(g10, 1, 2, 0, 0, PAIR)
+        quantise(b00, 0, 0)
         gather(g10, 1, 3, 0, 0, PAIR)
-        for h in range(2):
-            quantise(b01[h], 0, 2 + h)
-        b10 = [interleave(g10, h) for h in range(2)]
+        b10 = interleave(g10)
 
         g11 = new_g4()
         gather(g11, 1, 0, 1, 0, PAIR)
+        quantise(b01, 0, 1)
         gather(g11, 1, 1, 1, 0, PAIR)
         gather(g11, 1, 2, 1, 0, PAIR)
-        for h in range(2):
-            quantise(b10[h], 1, h)
+        quantise(b10, 1, 0)
         gather(g11, 1, 3, 1, 0, PAIR)
         y0 = products(0)
-        b11 = [interleave(g11, h) for h in range(2)]
+        b11 = interleave(g11)
 
         scatter(y0, 0, 0)
         scatter(y0, 0, 1)
-        for h in range(2):
-            quantise(b11[h], 1, 2 + h)
+        quantise(b11, 1, 1)
         y1 = products(1)
         scatter(y0, 0, 2)
         for kt in range(KT):

@@ -46,9 +46,9 @@ def tile_moe_bdx_lin_none_kernel(tc, dyT, w_words, w_scales, gate, offs, out):
 
         nc.vector.memset(wplanes[:].bitcast(I32), 0)
 
+        nc.scalar.dma_start(dy[0][0][:], dy_rows[0, 0])
         nc.sync.dma_start(offsets[:], offs)
         nc.sync.dma_start(gates[:, 0:FIRST], gate[0:P, 0:FIRST])
-        nc.sync.dma_start(dy[0][0][:], dy_rows[0, 0])
         nc.sync.dma_start(gates[:, FIRST:PAIR], gate[0:P, FIRST:PAIR])
         nc.sync.dma_start(gates[:, PAIR:T], gate[0:P, PAIR:T])
         for a in range(PASSES):
@@ -102,14 +102,14 @@ def tile_moe_bdx_lin_none_kernel(tc, dyT, w_words, w_scales, gate, offs, out):
             for kt in range(KT):
                 y = held.tile([P, PAIR], F32, name=f"y{pair}{kt}")
                 ys.append(y)
-                for half in range(2):
-                    e = 2 * pair + half
-                    cols = slice(e * C, (e + 1) * C)
-                    acc = psum.tile([P, C], F32, name="acc")
-                    for a in range(PASSES):
+                accs = [psum.tile([P, C], F32, name="acc") for half in range(2)]
+                for a in range(PASSES):
+                    for half in range(2):
+                        e = 2 * pair + half
+                        cols = slice(e * C, (e + 1) * C)
                         w0 = (e * PASSES + a) * K + P * kt
                         nc.tensor.matmul_mx(
-                            out=acc[:],
+                            out=accs[half][:],
                             lhsT=words[:, 2 * w0 : 2 * (w0 + P)].bitcast(FP4X4),
                             lhsT_scale=wplanes[:, w0 : w0 + P],
                             rhs=codes[a][:, cols].bitcast(FP8X4),
@@ -117,7 +117,8 @@ def tile_moe_bdx_lin_none_kernel(tc, dyT, w_words, w_scales, gate, offs, out):
                             start=(a == 0),
                             stop=(a == PASSES - 1),
                         )
-                    nc.scalar.copy(y[:, half * C : (half + 1) * C], acc[:])
+                for half in range(2):
+                    nc.scalar.copy(y[:, half * C : (half + 1) * C], accs[half][:])
             return ys
 
         def scatter(ys, pair, kt):
@@ -130,26 +131,29 @@ def tile_moe_bdx_lin_none_kernel(tc, dyT, w_words, w_scales, gate, offs, out):
         gather(g00, 0, 0, 0, 0, FIRST)
         gather(g00, 0, 0, 0, FIRST, PAIR)
         gather(g01, 0, 0, 1, 0, PAIR)
-        for t in range(1, PACK):
-            gather(g00, 0, t, 0, 0, PAIR)
-            gather(g01, 0, t, 1, 0, PAIR)
+        gather(g00, 0, 1, 0, 0, PAIR)
+        gather(g01, 0, 1, 1, 0, PAIR)
+        gather(g00, 0, 2, 0, 0, PAIR)
+        gather(g00, 0, 3, 0, 0, PAIR)
         b00 = interleave(g00)
+        gather(g01, 0, 2, 1, 0, PAIR)
+        gather(g01, 0, 3, 1, 0, PAIR)
         b01 = interleave(g01)
 
         g10 = new_g4()
         gather(g10, 1, 0, 0, 0, PAIR)
         gather(g10, 1, 1, 0, 0, PAIR)
         gather(g10, 1, 2, 0, 0, PAIR)
-        quantise(b00, 0, 0)
         gather(g10, 1, 3, 0, 0, PAIR)
         b10 = interleave(g10)
 
         g11 = new_g4()
         gather(g11, 1, 0, 1, 0, PAIR)
-        quantise(b01, 0, 1)
+        quantise(b00, 0, 0)
         gather(g11, 1, 1, 1, 0, PAIR)
-        gather(g11, 1, 2, 1, 0, PAIR)
+        quantise(b01, 0, 1)
         quantise(b10, 1, 0)
+        gather(g11, 1, 2, 1, 0, PAIR)
         gather(g11, 1, 3, 1, 0, PAIR)
         y0 = products(0)
         b11 = interleave(g11)

@@ -97,9 +97,9 @@ def tile_moe_bdx_lin_none_kernel(tc, dyT, w_words, w_scales, gate, offs, out):
             g4 = gath.tile([P, PACK, PAIR], F32, name="g4")
             return g4
 
-        def products(pair):
+        def products(pair, kts):
             ys = []
-            for kt in range(KT):
+            for kt in kts:
                 y = held.tile([P, PAIR], F32, name=f"y{pair}{kt}")
                 ys.append(y)
                 accs = [psum.tile([P, C], F32, name="acc") for half in range(2)]
@@ -136,32 +136,27 @@ def tile_moe_bdx_lin_none_kernel(tc, dyT, w_words, w_scales, gate, offs, out):
         gather(g00, 0, 2, 0, 0, PAIR)
         gather(g00, 0, 3, 0, 0, PAIR)
         b00 = interleave(g00)
+        g10 = new_g4()
+        for t in range(PACK):
+            gather(g10, 1, t, 0, 0, PAIR)
+        b10 = interleave(g10)
+        quantise(b00, 0, 0)
         gather(g01, 0, 2, 1, 0, PAIR)
         gather(g01, 0, 3, 1, 0, PAIR)
         b01 = interleave(g01)
-
-        g10 = new_g4()
-        gather(g10, 1, 0, 0, 0, PAIR)
-        gather(g10, 1, 1, 0, 0, PAIR)
-        gather(g10, 1, 2, 0, 0, PAIR)
-        gather(g10, 1, 3, 0, 0, PAIR)
-        b10 = interleave(g10)
-
-        g11 = new_g4()
-        gather(g11, 1, 0, 1, 0, PAIR)
-        quantise(b00, 0, 0)
-        gather(g11, 1, 1, 1, 0, PAIR)
-        quantise(b01, 0, 1)
         quantise(b10, 1, 0)
-        gather(g11, 1, 2, 1, 0, PAIR)
-        gather(g11, 1, 3, 1, 0, PAIR)
-        y0 = products(0)
+        y0 = products(0, (0,))
+        g11 = new_g4()
+        for t in range(PACK):
+            gather(g11, 1, t, 1, 0, PAIR)
+        quantise(b01, 0, 1)
         b11 = interleave(g11)
+        y0 += products(0, (1, 2))
 
         scatter(y0, 0, 0)
-        scatter(y0, 0, 1)
         quantise(b11, 1, 1)
-        y1 = products(1)
+        y1 = products(1, range(KT))
+        scatter(y0, 0, 1)
         scatter(y0, 0, 2)
         for kt in range(KT):
             scatter(y1, 1, kt)

from contextlib import ExitStack

import concourse.mybir as mybir

K, T, E, C, N = 384, 2048, 4, 512, 1024
FLOPS = 2 * K * N * E * C
BYTES = 4 * N * T + 2 * E * N * K // 4 + E * N // 32 * K + 4 * T + 2 * 128 * T // 16 + 4 * K * T

F32 = mybir.dt.float32
BF16 = mybir.dt.bfloat16
I32 = mybir.dt.int32
U32 = mybir.dt.uint32
U16 = mybir.dt.uint16
U8 = mybir.dt.uint8
FP8X4 = mybir.dt.float8_e5m2_x4
FP4X4 = mybir.dt.float4_e2m1fn_x4
MULT = mybir.AluOpType.mult

P = 128
PACK = 4
PASSES = N // (P * PACK)
KT = K // P
GROUPS = E * PASSES
PAIR = 2 * C
FIRST = 256
PAIRS = E // 2


def tile_moe_bdx_lin_none_kernel(tc, dyT, w_words, w_scales, gate, offs, out):
    nc = tc.nc
    with ExitStack() as ctx:
        held = ctx.enter_context(tc.tile_pool(name="held", bufs=1))
        gath = ctx.enter_context(tc.tile_pool(name="gath", bufs=3))
        psum = ctx.enter_context(tc.psum_pool(name="psum", bufs=8))

        offsets = held.tile([P, T // 16], U16, name="offsets")
        gates = held.tile([P, T], F32, name="gates")
        dy = [[held.tile([P, T], F32, name=f"dy{a}{t}") for t in range(PACK)] for a in range(PASSES)]
        words = held.tile([P, GROUPS * 2 * K], U8, name="words", align_bytes=64)
        wplanes = held.tile([P, GROUPS * K], U8, name="wplanes", align_bytes=64)
        outs = [held.tile([P, T], F32, name=f"outs{kt}") for kt in range(KT)]
        codes = [held.tile([P, T], U32, name=f"codes{a}", align_bytes=64) for a in range(PASSES)]
        planes = [held.tile([P, T], U8, name=f"planes{a}", align_bytes=64) for a in range(PASSES)]

        dy_rows = dyT.rearrange("(a p t) c -> a t p c", a=PASSES, p=P, t=PACK)

        nc.vector.memset(wplanes[:].bitcast(I32), 0)

        nc.scalar.dma_start(dy[0][0][:], dy_rows[0, 0])
        nc.sync.dma_start(offsets[:], offs)
        nc.sync.dma_start(gates[:, 0:FIRST], gate[0:P, 0:FIRST])
        nc.sync.dma_start(gates[:, FIRST:PAIR], gate[0:P, FIRST:PAIR])
        nc.sync.dma_start(gates[:, PAIR:T], gate[0:P, PAIR:T])
        for a in range(PASSES):
            for t in range(PACK):
                if a + t > 0:
                    nc.sync.dma_start(dy[a][t][:], dy_rows[a, t])
        nc.sync.dma_start(
            words[:].bitcast(I32).rearrange("p (g b) -> p g b", g=GROUPS),
            w_words.bitcast(I32).rearrange("e a p b -> p (e a) b"),
        )
        for q in range(4):
            nc.sync.dma_start(
                wplanes[32 * q : 32 * q + 4, :].bitcast(I32).rearrange("p (g k) -> p g k", g=GROUPS),
                w_scales.bitcast(I32).rearrange("e a f k -> f (e a) k")[4 * q : 4 * q + 4, :, :],
            )

        def gather(g4, a, t, pair, lo, hi):
            s0 = pair * PAIR + lo
            s1 = pair * PAIR + hi
            nc.vector.tensor_tensor(
                g4[:, t, lo:hi],
                dy[a][t][:].indirect(offsets[:, s0 // 16 : s1 // 16]),
                gates[:, s0:s1],
                MULT,
            )

        def interleave(g4):
            grouped = gath.tile([P, PAIR, PACK], BF16, name="grouped", bufs=3, align_bytes=64)
            for half in range(2):
                cols = slice(half * C, (half + 1) * C)
                nc.scalar.copy(
                    grouped[:, cols, :].rearrange("p (c i) t -> p c t i", i=4),
                    g4[:, :, cols].rearrange("p t (c i) -> p c t i", i=4),
                )
            return grouped

        def quantise(grouped, a, pair):
            cols = slice(pair * PAIR, (pair + 1) * PAIR)
            nc.vector.quantize_mx(
                out=codes[a][:, cols].bitcast(FP8X4),
                scales=planes[a][:, cols],
                in_=grouped[:].rearrange("p n t -> p (n t)"),
            )

        def new_g4():
            g4 = gath.tile([P, PACK, PAIR], F32, name="g4")
            return g4

        def products(pair, kts):
            ys = []
            for kt in kts:
                y = held.tile([P, PAIR], F32, name=f"y{pair}{kt}")
                ys.append(y)
                accs = [psum.tile([P, C], F32, name="acc") for half in range(2)]
                for a in range(PASSES):
                    for half in range(2):
                        e = 2 * pair + half
                        cols = slice(e * C, (e + 1) * C)
                        w0 = (e * PASSES + a) * K + P * kt
                        nc.tensor.matmul_mx(
                            out=accs[half][:],
                            lhsT=words[:, 2 * w0 : 2 * (w0 + P)].bitcast(FP4X4),
                            lhsT_scale=wplanes[:, w0 : w0 + P],
                            rhs=codes[a][:, cols].bitcast(FP8X4),
                            rhs_scale=planes[a][:, cols],
                            start=(a == 0),
                            stop=(a == PASSES - 1),
                        )
                for half in range(2):
                    nc.scalar.copy(y[:, half * C : (half + 1) * C], accs[half][:])
            return ys

        def scatter(ys, pair, kt):
            nc.vector.tensor_copy(
                outs[kt][:].indirect(offsets[:, pair * PAIR // 16 : (pair + 1) * PAIR // 16]), ys[kt][:]
            )

        g00 = new_g4()
        g01 = new_g4()
        gather(g00, 0, 0, 0, 0, FIRST)
        gather(g00, 0, 0, 0, FIRST, PAIR)
        gather(g01, 0, 0, 1, 0, PAIR)
        gather(g00, 0, 1, 0, 0, PAIR)
        gather(g01, 0, 1, 1, 0, PAIR)
        gather(g00, 0, 2, 0, 0, PAIR)
        gather(g00, 0, 3, 0, 0, PAIR)
        b00 = interleave(g00)
        g10 = new_g4()
        for t in range(PACK):
            gather(g10, 1, t, 0, 0, PAIR)
        b10 = interleave(g10)
        quantise(b00, 0, 0)
        gather(g01, 0, 2, 1, 0, PAIR)
        gather(g01, 0, 3, 1, 0, PAIR)
        b01 = interleave(g01)
        quantise(b10, 1, 0)
        y0 = products(0, (0,))
        g11 = new_g4()
        for t in range(PACK):
            gather(g11, 1, t, 1, 0, PAIR)
        quantise(b01, 0, 1)
        b11 = interleave(g11)
        y0 += products(0, (1, 2))

        scatter(y0, 0, 0)
        quantise(b11, 1, 1)
        y1 = products(1, range(KT))
        scatter(y0, 0, 1)
        scatter(y0, 0, 2)
        for kt in range(KT):
            scatter(y1, 1, kt)
            rows = slice(kt * P, (kt + 1) * P)
            nc.sync.dma_start(out[rows, 0:PAIR], outs[kt][:, 0:PAIR])
            nc.scalar.dma_start(out[rows, PAIR:T], outs[kt][:, PAIR:T])
